import numpy as np
import ml_dtypes


def mxq(x, axis, fmt="e4m3"):
    dtype, down = {"e4m3": (ml_dtypes.float8_e4m3fn, 7), "e5m2": (ml_dtypes.float8_e5m2, 14)}[fmt]
    v = np.moveaxis(np.asarray(x, np.float32).astype(ml_dtypes.bfloat16).astype(np.float64), axis, -1)
    blocks = v.reshape(v.shape[:-1] + (-1, 32))
    amax = np.abs(blocks).max(-1, keepdims=True)
    byte = np.maximum(np.where(amax > 0, np.frexp(amax)[1] - 1 + 127, 0) - down, 1)
    scale = np.exp2(byte - 127.0)
    codes = (blocks / scale).astype(np.float32).astype(dtype).astype(np.float64)
    return np.moveaxis((codes * scale).reshape(v.shape), -1, axis)


WIDE = False


def mx_kscale(k):
    if not WIDE:
        return np.ones(k)
    levels = np.array([10, -10, 5, -5, 0])
    if k % 512:
        return np.exp2(np.random.permutation(np.resize(levels, k // 32))).repeat(32)
    a = np.empty((k // 512, 16))
    for p in range(k // 512):
        a[p, :8] = np.random.permutation(np.resize(levels, 8))
        for g in range(8):
            far = levels[np.abs(levels - a[p, g]) >= 10]
            a[p, g + 8] = far[np.random.randint(len(far))]
    return np.exp2(a.ravel()).repeat(32)


def f64(x):
    return np.asarray(x).astype(np.float64)


def striped(idx):
    return np.tile(idx.reshape(-1, 16).T, (8, 1)).astype(np.uint16)


def unstriped(offs):
    return offs[:16].T.reshape(-1).astype(np.int64)


E2M1 = np.array([0.0, 0.5, 1.0, 1.5, 2.0, 3.0, 4.0, 6.0, -0.0, -0.5, -1.0, -1.5, -2.0, -3.0, -4.0, -6.0])


def pack_weight(w, fmt):
    k, n = w.shape
    w = f64(np.asarray(w, np.float32).astype(ml_dtypes.bfloat16)).reshape(k // 32, 32, n)
    amax = np.abs(w).max(1)
    if fmt == "e4m3":
        byte = np.frexp(amax)[1] - 1 + 127 - 7
    else:
        mant, ex = np.frexp(amax / 6.0)
        byte = np.where(mant > 0.5, ex, ex - 1) + 127
    byte = np.clip(np.where(amax > 0, byte, 1), 1, 254)
    scaled = (w * np.exp2(127.0 - byte)[:, None, :]).reshape(k, n).astype(np.float32)
    by_word = np.ascontiguousarray(scaled.reshape(k // 512, 128, 4, n).transpose(0, 1, 3, 2))
    if fmt == "e4m3":
        words = by_word.astype(ml_dtypes.float8_e4m3fn).view(np.uint8)
    else:
        c = by_word.astype(ml_dtypes.float4_e2m1fn).view(np.uint8) & 0xF
        words = (c[..., 0::2] | (c[..., 1::2] << 4)).reshape(k // 512, 128, 2 * n)
    return np.ascontiguousarray(words), np.ascontiguousarray(byte.astype(np.uint8).reshape(k // 512, 16, n))


def unpack_weight(words, scales, fmt):
    g, _, n = scales.shape
    words = np.ascontiguousarray(words).reshape(g, 128, n, -1)
    if fmt == "e4m3":
        vals = words.view(ml_dtypes.float8_e4m3fn).astype(np.float64)
    else:
        nib = np.empty((g, 128, n, 4), np.uint8)
        nib[..., 0::2] = words & 0xF
        nib[..., 1::2] = words >> 4
        vals = E2M1[nib]
    vals = vals * np.repeat(np.exp2(scales.astype(np.float64) - 127.0), 8, axis=1)[..., None]
    return vals.transpose(0, 1, 3, 2).reshape(g * 512, n)


K, T, E, C, N = 1536, 1536, 12, 128, 128
TOP = 3
PAD = 64
K8 = 512


def by_expert(wq, xq):
    return np.concatenate([wq[e].T @ xq[:, e * C:(e + 1) * C] for e in range(E)], axis=1)


def setup_inputs():
    n = np.random.standard_normal
    s = mx_kscale(K)[:, None]
    slot_token = np.empty(E * C, np.int64); pos = np.tile(E * C + np.arange(T) % PAD, (TOP, 1)); taken = np.zeros(T, np.int64)
    liked = np.random.randn(T)
    for e in np.random.permutation(E):
        free = np.flatnonzero(taken < TOP); pick = np.random.permutation(free[np.argsort(-(liked[free] + np.random.gumbel(size=free.size)))[:C]]); slot_token[e * C:(e + 1) * C] = pick
        pos[taken[pick], pick] = e * C + np.arange(C); taken[pick] += 1
    g = np.random.uniform(0.2, 0.8, (TOP, T))
    w = n((E, K, N)) / np.sqrt(K) / s[None]
    w8 = [pack_weight(m[:K8], "e4m3") for m in w]
    w4 = [pack_weight(m[K8:], "e2m1") for m in w]
    return {
        "xT": (n((K, T)) * s).astype(np.float32),
        "w8_words": np.stack([m[0] for m in w8]),
        "w8_scales": np.stack([m[1] for m in w8]),
        "w4_words": np.stack([m[0] for m in w4]),
        "w4_scales": np.stack([m[1] for m in w4]),
        "gate": np.stack([np.tile(r, (N, 1)) for r in g]).astype(np.float32),
        "offs": striped(slot_token),
        "pos1": striped(pos[0]),
        "pos2": striped(pos[1]),
        "pos3": striped(pos[2]),
    }


def reference(xT, w8_words, w8_scales, w4_words, w4_scales, gate, offs, pos1, pos2, pos3):
    idx = unstriped(offs)
    w = np.stack([np.concatenate([unpack_weight(w8_words[e], w8_scales[e], "e4m3"), unpack_weight(w4_words[e], w4_scales[e], "e2m1")]) for e in range(E)])
    xq = mxq(f64(xT)[:, idx], 0, "e4m3")
    y = by_expert(w, xq)
    y = np.concatenate([y, np.zeros((N, PAD))], axis=1)
    return sum(f64(gate[r]) * y[:, unstriped(p)] for r, p in enumerate((pos1, pos2, pos3)))

@@ -1,0 +1,173 @@
+from contextlib import ExitStack
+
+import concourse.mybir as mybir
+
+K, T, E, C, N = 1536, 1536, 12, 128, 128
+TOP = 3
+PAD = 64
+S = E * C
+P = 128
+PACK = 4
+K_PASS = P * PACK
+
+F32 = mybir.dt.float32
+BF16 = mybir.dt.bfloat16
+I32 = mybir.dt.int32
+U32 = mybir.dt.uint32
+U16 = mybir.dt.uint16
+U8 = mybir.dt.uint8
+FP8X4 = mybir.dt.float8_e4m3fn_x4
+FP4X4 = mybir.dt.float4_e2m1fn_x4
+MULT = mybir.AluOpType.mult
+ADD = mybir.AluOpType.add
+
+FLOPS = 2 * K * S * N
+
+PASS_ORDER = (1, 0, 2)
+LOADS = (
+    ((("v", 512), ("s", 256)), (("v", 256), ("s", 256)), (("v", 128), ("s", 128))),
+    ((("s", 256), ("s", 512)), (("s", 512),), (("s", 256),)),
+    ((("s", 256), ("s", 512)), (("s", 256), ("v", 256)), (("s", 128), ("v", 128))),
+)
+EARLY_SLOTS = (768, 768)
+LATE_EXPERTS = (4, 4, 2, 2)
+TOKEN_CHUNKS = (512, 512, 256, 256)
+
+
+def runs(sizes):
+    start = 0
+    result = []
+    for size in sizes:
+        result.append((start, start + size))
+        start = start + size
+    return result
+
+
+def tile_moe_ecr_lin_none_kernel(
+    tc, xT, w8_words, w8_scales, w4_words, w4_scales, gate, offs, pos1, pos2, pos3, out
+):
+    nc = tc.nc
+    with ExitStack() as ctx:
+        lists = ctx.enter_context(tc.tile_pool(name="lists", bufs=1))
+        keep = ctx.enter_context(tc.tile_pool(name="keep", bufs=1))
+        psum = ctx.enter_context(tc.psum_pool(name="psum", bufs=1))
+
+        w8s = keep.tile([P, E, N], U8, name="w8s", align_bytes=64)
+        w4s = keep.tile([P, 2 * E, N], U8, name="w4s", align_bytes=64)
+        planes = [keep.tile([P, T], U8, name=f"plane{i}", align_bytes=64) for i in range(2)]
+        y = keep.tile([P, S + PAD], F32, name="y")
+        nc.vector.memset(w4s[:].bitcast(I32), 0)
+        nc.vector.memset(w8s[:].bitcast(I32), 0)
+        for plane in planes:
+            nc.vector.memset(plane[:].bitcast(I32), 0)
+        nc.vector.memset(y[:, S:], 0.0)
+
+        plane_of = {1: (0, 0), 0: (1, 4), 2: (1, 0)}
+        codes = [keep.tile([P, T], U32, name=f"codes{a}", align_bytes=64) for a in range(3)]
+        slot_codes = [keep.tile([P, S], U32, name=f"slot_codes{a}", align_bytes=64) for a in range(3)]
+        slot_planes = [keep.tile([P, S], U8, name=f"slot_plane{i}", align_bytes=64) for i in range(2)]
+        offs_sb = lists.tile([P, S // 16], U16, name="offs_sb")
+        pos_sb = [lists.tile([P, T // 16], U16, name=f"pos_sb{r}") for r in range(TOP)]
+
+        def gather(dst, src, s0, s1):
+            nc.vector.tensor_copy(dst[:, s0:s1], src[:].indirect(offs_sb[:, s0 // 16 : s1 // 16]))
+
+        raws = {}
+        for i, a in enumerate(PASS_ORDER):
+            rows = xT[a * K_PASS : (a + 1) * K_PASS, :].rearrange("(p j) t -> p j t", j=PACK)
+            for c, (t0, t1) in enumerate(runs([sum(w for _, w in load) for load in LOADS[i]])):
+                raw = keep.tile([P, PACK, t1 - t0], F32, name=f"raw{a}_{c}")
+                nc.sync.dma_start(out=raw[:], in_=rows[:, :, t0:t1])
+                raws[a, c] = (raw, t0)
+            if i == 0:
+                nc.sync.dma_start(offs_sb[:], offs)
+
+        w8_rows = w8_scales.rearrange("e a (q r) n -> r q (e a) n", r=4)
+        w4_rows = w4_scales.rearrange("e a (q r) n -> r q (e a) n", r=4)
+        for r in range(4):
+            nc.sync.dma_start(out=w4s[:].bitcast(I32)[r:P:32], in_=w4_rows[r].bitcast(I32))
+            nc.sync.dma_start(out=w8s[:].bitcast(I32)[r:P:32], in_=w8_rows[r].bitcast(I32))
+        w8 = []
+        w4 = []
+        for g, (e0, e1) in enumerate(runs(LATE_EXPERTS)):
+            w8_g = keep.tile([P, e1 - e0, 4 * N], U8, name=f"w8_{g}", align_bytes=64)
+            w4_g = keep.tile([P, 2 * (e1 - e0), 2 * N], U8, name=f"w4_{g}", align_bytes=64)
+            nc.sync.dma_start(
+                out=w4_g[:].bitcast(I32), in_=w4_words[e0:e1].rearrange("e a p b -> p (e a) b").bitcast(I32)
+            )
+            nc.sync.dma_start(
+                out=w8_g[:].bitcast(I32), in_=w8_words[e0:e1].rearrange("e a p n r -> p (e a) (n r)").bitcast(I32)
+            )
+            w8.append(w8_g)
+            w4.append(w4_g)
+        for tile, pos in zip(pos_sb, (pos1, pos2, pos3)):
+            nc.sync.dma_start(tile[:], pos)
+        gates = {}
+        for c, (t0, t1) in enumerate(runs(TOKEN_CHUNKS)):
+            for r in range(TOP):
+                g_sb = keep.tile([P, t1 - t0], F32, name=f"gate{r}_{c}")
+                nc.sync.dma_start(out=g_sb[:], in_=gate[r, :, t0:t1])
+                gates[r, c] = g_sb
+
+        for i, a in enumerate(PASS_ORDER):
+            which, first = plane_of[a]
+            for c, load in enumerate(LOADS[i]):
+                raw, base = raws[a, c]
+                for (engine, width), (u0, u1) in zip(load, runs([w for _, w in load])):
+                    grouped = keep.tile([P, width * PACK], BF16, name=f"grouped{a}_{c}_{u0}", align_bytes=64)
+                    dst = grouped[:].rearrange("p (c i j) -> p c j i", i=4, j=PACK)
+                    src = raw[:, :, u0:u1].rearrange("p j (c i) -> p c j i", i=4)
+                    if engine == "v":
+                        nc.vector.tensor_copy(out=dst, in_=src)
+                    else:
+                        nc.scalar.copy(out=dst, in_=src)
+                    nc.vector.quantize_mx(
+                        out=codes[a][:, base + u0 : base + u1].bitcast(FP8X4),
+                        scales=planes[which][first:P, base + u0 : base + u1],
+                        in_=grouped[:],
+                    )
+            if i < 2:
+                for s0, s1 in runs(EARLY_SLOTS):
+                    gather(slot_codes[a], codes[a], s0, s1)
+            if i == 0:
+                for s0, s1 in runs(EARLY_SLOTS):
+                    gather(slot_planes[0], planes[0], s0, s1)
+
+        last = PASS_ORDER[2]
+        for g, (e0, e1) in enumerate(runs(LATE_EXPERTS)):
+            gather(slot_planes[1], planes[1], e0 * C, e1 * C)
+            gather(slot_codes[last], codes[last], e0 * C, e1 * C)
+            acc = psum.tile([P, (e1 - e0) * C], F32, name=f"acc{g}")
+            for e in range(e0, e1):
+                cols = slice(e * C, (e + 1) * C)
+                for i, a in enumerate(PASS_ORDER):
+                    which, first = plane_of[a]
+                    if a == 0:
+                        lhsT = w8[g][:, e - e0, :].bitcast(FP8X4)
+                        lhsT_scale = w8s[:, e, :]
+                    else:
+                        lhsT = w4[g][:, 2 * (e - e0) + a - 1, :].bitcast(FP4X4)
+                        lhsT_scale = w4s[:, 2 * e + a - 1, :]
+                    nc.tensor.matmul_mx(
+                        out=acc[:, (e - e0) * C : (e - e0 + 1) * C],
+                        lhsT=lhsT,
+                        lhsT_scale=lhsT_scale,
+                        rhs=slot_codes[a][:, cols].bitcast(FP8X4),
+                        rhs_scale=slot_planes[which][first:P, cols],
+                        start=(i == 0),
+                        stop=(i == 2),
+                    )
+            nc.scalar.copy(out=y[:, e0 * C : e1 * C], in_=acc[:])
+
+        for c, (t0, t1) in enumerate(runs(TOKEN_CHUNKS)):
+            terms = []
+            for r in range(TOP):
+                term = keep.tile([P, t1 - t0], F32, name=f"term{r}_{c}")
+                nc.vector.tensor_tensor(
+                    term[:], y[:].indirect(pos_sb[r][:, t0 // 16 : t1 // 16]), gates[r, c][:], MULT
+                )
+                terms.append(term)
+            pair = keep.tile([P, t1 - t0], F32, name=f"pair{c}")
+            nc.vector.tensor_tensor(pair[:], terms[0][:], terms[1][:], ADD)
+            nc.vector.tensor_tensor(terms[0][:], pair[:], terms[2][:], ADD)
+            nc.sync.dma_start(out=out[:, t0:t1], in_=terms[0][:])

@@ -1,6 +1,7 @@
 from contextlib import ExitStack
 
 import concourse.mybir as mybir
+from concourse.masks import make_identity
 
 K, T, E, C, N = 1536, 1536, 12, 128, 128
 TOP = 3
@@ -25,9 +26,9 @@ FLOPS = 2 * K * S * N
 
 PASS_ORDER = (1, 0, 2)
 LOADS = (
-    ((("v", 512), ("s", 256)), (("v", 256), ("s", 256)), (("v", 128), ("s", 128))),
-    ((("s", 256), ("s", 512)), (("s", 512),), (("s", 256),)),
-    ((("s", 256), ("s", 512)), (("s", 256), ("v", 256)), (("s", 128), ("v", 128))),
+    ((("v", 256), ("s", 256)), (("v", 256), ("s", 256)), (("v", 128), ("s", 128)), (("v", 128), ("s", 128))),
+    ((("s", 256),), (("s", 512),), (("s", 512),), (("s", 256),)),
+    ((("s", 512),), (("s", 512),), (("s", 256),), (("s", 128), ("s", 128))),
 )
 EARLY_SLOTS = (768, 768)
 LATE_EXPERTS = (4, 4, 2, 2)
@@ -61,6 +62,9 @@ def tile_moe_ecr_lin_none_kernel(
         for plane in planes:
             nc.vector.memset(plane[:].bitcast(I32), 0)
         nc.vector.memset(y[:, S:], 0.0)
+
+        ident = keep.tile([P, P], F32, name="ident")
+        make_identity(nc, ident[:])
 
         plane_of = {1: (0, 0), 0: (1, 4), 2: (1, 0)}
         codes = [keep.tile([P, T], U32, name=f"codes{a}", align_bytes=64) for a in range(3)]
@@ -133,41 +137,79 @@ def tile_moe_ecr_lin_none_kernel(
                 for s0, s1 in runs(EARLY_SLOTS):
                     gather(slot_planes[0], planes[0], s0, s1)
 
+        def product(acc, g, e, i):
+            a = PASS_ORDER[i]
+            which, first = plane_of[a]
+            e0 = runs(LATE_EXPERTS)[g][0]
+            cols = slice(e * C, (e + 1) * C)
+            if a == 0:
+                lhsT = w8[g][:, e - e0, :].bitcast(FP8X4)
+                lhsT_scale = w8s[:, e, :]
+            else:
+                lhsT = w4[g][:, 2 * (e - e0) + a - 1, :].bitcast(FP4X4)
+                lhsT_scale = w4s[:, 2 * e + a - 1, :]
+            nc.tensor.matmul_mx(
+                out=acc,
+                lhsT=lhsT,
+                lhsT_scale=lhsT_scale,
+                rhs=slot_codes[a][:, cols].bitcast(FP8X4),
+                rhs_scale=slot_planes[which][first:P, cols],
+                start=(i == 0),
+                stop=(i == 2),
+            )
+
         last = PASS_ORDER[2]
         for g, (e0, e1) in enumerate(runs(LATE_EXPERTS)):
             gather(slot_planes[1], planes[1], e0 * C, e1 * C)
             gather(slot_codes[last], codes[last], e0 * C, e1 * C)
-            acc = psum.tile([P, (e1 - e0) * C], F32, name=f"acc{g}")
-            for e in range(e0, e1):
-                cols = slice(e * C, (e + 1) * C)
-                for i, a in enumerate(PASS_ORDER):
-                    which, first = plane_of[a]
-                    if a == 0:
-                        lhsT = w8[g][:, e - e0, :].bitcast(FP8X4)
-                        lhsT_scale = w8s[:, e, :]
-                    else:
-                        lhsT = w4[g][:, 2 * (e - e0) + a - 1, :].bitcast(FP4X4)
-                        lhsT_scale = w4s[:, 2 * e + a - 1, :]
-                    nc.tensor.matmul_mx(
-                        out=acc[:, (e - e0) * C : (e - e0 + 1) * C],
-                        lhsT=lhsT,
-                        lhsT_scale=lhsT_scale,
-                        rhs=slot_codes[a][:, cols].bitcast(FP8X4),
-                        rhs_scale=slot_planes[which][first:P, cols],
-                        start=(i == 0),
-                        stop=(i == 2),
-                    )
-            nc.scalar.copy(out=y[:, e0 * C : e1 * C], in_=acc[:])
+            if e1 < E:
+                acc = psum.tile([P, (e1 - e0) * C], F32, name=f"acc{g}", tag=f"acc{g}")
+                for e in range(e0, e1):
+                    for i in range(3):
+                        product(acc[:, (e - e0) * C : (e - e0 + 1) * C], g, e, i)
+                nc.scalar.copy(out=y[:, e0 * C : e1 * C], in_=acc[:])
+            else:
+                own = [psum.tile([P, C], F32, name=f"own{e}") for e in range(e0, e1)]
+                for i in range(3):
+                    for e in range(e0, e1):
+                        product(own[e - e0][:], g, e, i)
+                nc.vector.tensor_copy(out=y[:, e0 * C : (e0 + 1) * C], in_=own[0][:])
+                nc.scalar.copy(out=y[:, (e0 + 1) * C : e1 * C], in_=own[1][:])
+
+        def turn(bank, block, r):
+            nc.tensor.matmul(bank, lhsT=block, rhs=ident[:], is_transpose=True, start=(r == 0), stop=(r == TOP - 1))
 
         for c, (t0, t1) in enumerate(runs(TOKEN_CHUNKS)):
+            width = t1 - t0
             terms = []
             for r in range(TOP):
-                term = keep.tile([P, t1 - t0], F32, name=f"term{r}_{c}")
+                term = keep.tile([P, width], F32, name=f"term{r}_{c}")
                 nc.vector.tensor_tensor(
                     term[:], y[:].indirect(pos_sb[r][:, t0 // 16 : t1 // 16]), gates[r, c][:], MULT
                 )
                 terms.append(term)
-            pair = keep.tile([P, t1 - t0], F32, name=f"pair{c}")
-            nc.vector.tensor_tensor(pair[:], terms[0][:], terms[1][:], ADD)
-            nc.vector.tensor_tensor(terms[0][:], pair[:], terms[2][:], ADD)
-            nc.sync.dma_start(out=out[:, t0:t1], in_=terms[0][:])
+            total = keep.tile([P, width], F32, name=f"total{c}")
+            if t1 < T:
+                turned_sb = keep.tile([P, width], F32, name=f"turned_sb{c}")
+                if c + 2 < len(TOKEN_CHUNKS):
+                    turned = psum.tile([P, width], F32, name="turned", tag="turned", bufs=2)
+                    for b in range(0, width, P):
+                        for r in range(TOP):
+                            turn(turned[:, b : b + P], terms[r][:, b : b + P], r)
+                    nc.scalar.copy(out=turned_sb[:], in_=turned[:])
+                else:
+                    banks = [psum.tile([P, P], F32, name=f"turned{b}", tag=f"acc{b}") for b in range(width // P)]
+                    for r in range(TOP):
+                        for b, bank in enumerate(banks):
+                            turn(bank[:], terms[r][:, b * P : (b + 1) * P], r)
+                    for b, bank in enumerate(banks):
+                        nc.scalar.copy(out=turned_sb[:, b * P : (b + 1) * P], in_=bank[:])
+                back = psum.tile([P, width], F32, name="back", tag="back", bufs=1)
+                for b in range(0, width, P):
+                    nc.tensor.transpose(back[:, b : b + P], turned_sb[:, b : b + P], ident[:])
+                nc.scalar.copy(out=total[:], in_=back[:])
+            else:
+                pair = keep.tile([P, width], F32, name="pair")
+                nc.vector.tensor_tensor(pair[:], terms[0][:], terms[1][:], ADD)
+                nc.vector.tensor_tensor(total[:], pair[:], terms[2][:], ADD)
+            nc.sync.dma_start(out=out[:, t0:t1], in_=total[:])

@@ -26,9 +26,9 @@ FLOPS = 2 * K * S * N
 
 PASS_ORDER = (1, 0, 2)
 LOADS = (
-    ((("v", 256), ("s", 256)), (("v", 256), ("s", 256)), (("v", 128), ("s", 128)), (("v", 128), ("s", 128))),
-    ((("s", 256),), (("s", 512),), (("s", 512),), (("s", 256),)),
-    ((("s", 512),), (("s", 512),), (("s", 256),), (("s", 128), ("s", 128))),
+    ((("s", 512), ("v", 256)), (("v", 256), ("s", 256)), (("v", 128), ("s", 128))),
+    ((("s", 512),), (("s", 512),), (("s", 512),)),
+    ((("s", 512),), (("s", 512),), (("s", 256), ("v", 256))),
 )
 EARLY_SLOTS = (768, 768)
 LATE_EXPERTS = (4, 4, 2, 2)
@@ -51,14 +51,12 @@ def tile_moe_ecr_lin_none_kernel(
     with ExitStack() as ctx:
         lists = ctx.enter_context(tc.tile_pool(name="lists", bufs=1))
         keep = ctx.enter_context(tc.tile_pool(name="keep", bufs=1))
-        psum = ctx.enter_context(tc.psum_pool(name="psum", bufs=1))
+        psum = ctx.enter_context(tc.psum_pool(name="psum", bufs=8))
 
-        w8s = keep.tile([P, E, N], U8, name="w8s", align_bytes=64)
-        w4s = keep.tile([P, 2 * E, N], U8, name="w4s", align_bytes=64)
+        ws = keep.tile([P, 3 * E * N], U8, name="ws", align_bytes=64)
         planes = [keep.tile([P, T], U8, name=f"plane{i}", align_bytes=64) for i in range(2)]
         y = keep.tile([P, S + PAD], F32, name="y")
-        nc.vector.memset(w4s[:].bitcast(I32), 0)
-        nc.vector.memset(w8s[:].bitcast(I32), 0)
+        nc.vector.memset(ws[:].bitcast(I32), 0)
         for plane in planes:
             nc.vector.memset(plane[:].bitcast(I32), 0)
         nc.vector.memset(y[:, S:], 0.0)
@@ -86,11 +84,10 @@ def tile_moe_ecr_lin_none_kernel(
             if i == 0:
                 nc.sync.dma_start(offs_sb[:], offs)
 
-        w8_rows = w8_scales.rearrange("e a (q r) n -> r q (e a) n", r=4)
-        w4_rows = w4_scales.rearrange("e a (q r) n -> r q (e a) n", r=4)
-        for r in range(4):
-            nc.sync.dma_start(out=w4s[:].bitcast(I32)[r:P:32], in_=w4_rows[r].bitcast(I32))
-            nc.sync.dma_start(out=w8s[:].bitcast(I32)[r:P:32], in_=w8_rows[r].bitcast(I32))
+        ws_words = ws[:].bitcast(I32)
+        ws_cols = ws_words.rearrange("p (m n) -> p m n", n=N // 4)
+        nc.sync.dma_start(out=ws_cols[0:16, E:, :], in_=w4_scales.rearrange("e a q n -> q (e a) n").bitcast(I32))
+        nc.sync.dma_start(out=ws_cols[0:16, :E, :], in_=w8_scales.rearrange("e a q n -> q (e a) n").bitcast(I32))
         w8 = []
         w4 = []
         for g, (e0, e1) in enumerate(runs(LATE_EXPERTS)):
@@ -144,10 +141,10 @@ def tile_moe_ecr_lin_none_kernel(
             cols = slice(e * C, (e + 1) * C)
             if a == 0:
                 lhsT = w8[g][:, e - e0, :].bitcast(FP8X4)
-                lhsT_scale = w8s[:, e, :]
+                lhsT_scale = ws[:, e * N : (e + 1) * N]
             else:
                 lhsT = w4[g][:, 2 * (e - e0) + a - 1, :].bitcast(FP4X4)
-                lhsT_scale = w4s[:, 2 * e + a - 1, :]
+                lhsT_scale = ws[:, (E + 2 * e + a - 1) * N : (E + 2 * e + a) * N]
             nc.tensor.matmul_mx(
                 out=acc,
                 lhsT=lhsT,
@@ -158,18 +155,21 @@ def tile_moe_ecr_lin_none_kernel(
                 stop=(i == 2),
             )
 
+        for q in range(1, 4):
+            nc.scalar.dma_start(out=ws_words[32 * q : 32 * q + 4, :], in_=ws_words[4 * q : 4 * q + 4, :])
+
         last = PASS_ORDER[2]
         for g, (e0, e1) in enumerate(runs(LATE_EXPERTS)):
             gather(slot_planes[1], planes[1], e0 * C, e1 * C)
             gather(slot_codes[last], codes[last], e0 * C, e1 * C)
             if e1 < E:
-                acc = psum.tile([P, (e1 - e0) * C], F32, name=f"acc{g}", tag=f"acc{g}")
+                acc = psum.tile([P, (e1 - e0) * C], F32, name=f"acc{g}", tag="bank")
                 for e in range(e0, e1):
                     for i in range(3):
                         product(acc[:, (e - e0) * C : (e - e0 + 1) * C], g, e, i)
                 nc.scalar.copy(out=y[:, e0 * C : e1 * C], in_=acc[:])
             else:
-                own = [psum.tile([P, C], F32, name=f"own{e}") for e in range(e0, e1)]
+                own = [psum.tile([P, C], F32, name=f"own{e}", tag="bank") for e in range(e0, e1)]
                 for i in range(3):
                     for e in range(e0, e1):
                         product(own[e - e0][:], g, e, i)
@@ -191,20 +191,13 @@ def tile_moe_ecr_lin_none_kernel(
             total = keep.tile([P, width], F32, name=f"total{c}")
             if t1 < T:
                 turned_sb = keep.tile([P, width], F32, name=f"turned_sb{c}")
-                if c + 2 < len(TOKEN_CHUNKS):
-                    turned = psum.tile([P, width], F32, name="turned", tag="turned", bufs=2)
-                    for b in range(0, width, P):
-                        for r in range(TOP):
-                            turn(turned[:, b : b + P], terms[r][:, b : b + P], r)
-                    nc.scalar.copy(out=turned_sb[:], in_=turned[:])
-                else:
-                    banks = [psum.tile([P, P], F32, name=f"turned{b}", tag=f"acc{b}") for b in range(width // P)]
-                    for r in range(TOP):
-                        for b, bank in enumerate(banks):
-                            turn(bank[:], terms[r][:, b * P : (b + 1) * P], r)
+                banks = [psum.tile([P, P], F32, name=f"turned{b}", tag="bank") for b in range(width // P)]
+                for r in range(TOP):
                     for b, bank in enumerate(banks):
-                        nc.scalar.copy(out=turned_sb[:, b * P : (b + 1) * P], in_=bank[:])
-                back = psum.tile([P, width], F32, name="back", tag="back", bufs=1)
+                        turn(bank[:], terms[r][:, b * P : (b + 1) * P], r)
+                for b, bank in enumerate(banks):
+                    nc.scalar.copy(out=turned_sb[:, b * P : (b + 1) * P], in_=bank[:])
+                back = psum.tile([P, width], F32, name="back", tag="bank")
                 for b in range(0, width, P):
                     nc.tensor.transpose(back[:, b : b + P], turned_sb[:, b : b + P], ident[:])
                 nc.scalar.copy(out=total[:], in_=back[:])

@@ -10,6 +10,12 @@ S = E * C
 P = 128
 PACK = 4
 K_PASS = P * PACK
+PASSES = K // K_PASS
+STRIPE = 16
+QUADRANT = 32
+SCALE_ROWS = 4
+LINE = 4
+BANKS = 8
 
 F32 = mybir.dt.float32
 BF16 = mybir.dt.bfloat16
@@ -25,14 +31,16 @@ ADD = mybir.AluOpType.add
 FLOPS = 2 * K * S * N
 
 PASS_ORDER = (1, 0, 2)
+PLANE_OF = {1: (0, 0), 0: (1, SCALE_ROWS), 2: (1, 0)}
+
 LOADS = (
-    ((("s", 512), ("v", 256)), (("v", 256), ("s", 256)), (("v", 128), ("s", 128))),
-    ((("s", 512),), (("s", 512),), (("s", 512),)),
-    ((("s", 512),), (("s", 512),), (("s", 256), ("v", 256))),
+    ((("vector", 512), ("scalar", 256)), (("vector", 256), ("scalar", 256)), (("vector", 128), ("scalar", 128))),
+    ((("scalar", 512),), (("scalar", 512),), (("scalar", 256), ("scalar", 256))),
+    ((("scalar", 512),), (("scalar", 512),), (("vector", 256), ("scalar", 256))),
 )
-EARLY_SLOTS = (768, 768)
-LATE_EXPERTS = (4, 4, 2, 2)
-TOKEN_CHUNKS = (512, 512, 256, 256)
+EARLY_SLOTS = (S // 2, S // 2)
+EXPERT_GROUPS = (4, 4, 2, 2)
+TOKEN_STEPS = (512, 512, 256, 256)
 
 
 def runs(sizes):
@@ -44,6 +52,10 @@ def runs(sizes):
     return result
 
 
+def entries(list_tile, start, stop):
+    return list_tile[:, start // STRIPE : stop // STRIPE]
+
+
 def tile_moe_ecr_lin_none_kernel(
     tc, xT, w8_words, w8_scales, w4_words, w4_scales, gate, offs, pos1, pos2, pos3, out
 ):
@@ -51,12 +63,14 @@ def tile_moe_ecr_lin_none_kernel(
     with ExitStack() as ctx:
         lists = ctx.enter_context(tc.tile_pool(name="lists", bufs=1))
         keep = ctx.enter_context(tc.tile_pool(name="keep", bufs=1))
-        psum = ctx.enter_context(tc.psum_pool(name="psum", bufs=8))
+        psum = ctx.enter_context(tc.psum_pool(name="psum", bufs=BANKS))
 
-        ws = keep.tile([P, 3 * E * N], U8, name="ws", align_bytes=64)
+        w8_plane = keep.tile([P, E, N], U8, name="w8_plane", align_bytes=64)
+        w4_plane = keep.tile([P, 2 * E, N], U8, name="w4_plane", align_bytes=64)
         planes = [keep.tile([P, T], U8, name=f"plane{i}", align_bytes=64) for i in range(2)]
         y = keep.tile([P, S + PAD], F32, name="y")
-        nc.vector.memset(ws[:].bitcast(I32), 0)
+        nc.vector.memset(w4_plane[:].bitcast(I32), 0)
+        nc.vector.memset(w8_plane[:].bitcast(I32), 0)
         for plane in planes:
             nc.vector.memset(plane[:].bitcast(I32), 0)
         nc.vector.memset(y[:, S:], 0.0)
@@ -64,33 +78,32 @@ def tile_moe_ecr_lin_none_kernel(
         ident = keep.tile([P, P], F32, name="ident")
         make_identity(nc, ident[:])
 
-        plane_of = {1: (0, 0), 0: (1, 4), 2: (1, 0)}
-        codes = [keep.tile([P, T], U32, name=f"codes{a}", align_bytes=64) for a in range(3)]
-        slot_codes = [keep.tile([P, S], U32, name=f"slot_codes{a}", align_bytes=64) for a in range(3)]
+        codes = [keep.tile([P, T], U32, name=f"codes{a}", align_bytes=64) for a in range(PASSES)]
+        slot_codes = [keep.tile([P, S], U32, name=f"slot_codes{a}", align_bytes=64) for a in range(PASSES)]
         slot_planes = [keep.tile([P, S], U8, name=f"slot_plane{i}", align_bytes=64) for i in range(2)]
-        offs_sb = lists.tile([P, S // 16], U16, name="offs_sb")
-        pos_sb = [lists.tile([P, T // 16], U16, name=f"pos_sb{r}") for r in range(TOP)]
-
-        def gather(dst, src, s0, s1):
-            nc.vector.tensor_copy(dst[:, s0:s1], src[:].indirect(offs_sb[:, s0 // 16 : s1 // 16]))
+        offs_sb = lists.tile([P, S // STRIPE], U16, name="offs_sb")
+        pos_sb = [lists.tile([P, T // STRIPE], U16, name=f"pos_sb{r}") for r in range(TOP)]
 
         raws = {}
-        for i, a in enumerate(PASS_ORDER):
+        for step, a in enumerate(PASS_ORDER):
             rows = xT[a * K_PASS : (a + 1) * K_PASS, :].rearrange("(p j) t -> p j t", j=PACK)
-            for c, (t0, t1) in enumerate(runs([sum(w for _, w in load) for load in LOADS[i]])):
+            sizes = [sum(tokens for engine, tokens in load) for load in LOADS[step]]
+            for c, (t0, t1) in enumerate(runs(sizes)):
                 raw = keep.tile([P, PACK, t1 - t0], F32, name=f"raw{a}_{c}")
                 nc.sync.dma_start(out=raw[:], in_=rows[:, :, t0:t1])
                 raws[a, c] = (raw, t0)
-            if i == 0:
+            if step == 0:
                 nc.sync.dma_start(offs_sb[:], offs)
 
-        ws_words = ws[:].bitcast(I32)
-        ws_cols = ws_words.rearrange("p (m n) -> p m n", n=N // 4)
-        nc.sync.dma_start(out=ws_cols[0:16, E:, :], in_=w4_scales.rearrange("e a q n -> q (e a) n").bitcast(I32))
-        nc.sync.dma_start(out=ws_cols[0:16, :E, :], in_=w8_scales.rearrange("e a q n -> q (e a) n").bitcast(I32))
+        w8_rows = w8_scales.rearrange("e a (q r) n -> r q (e a) n", r=SCALE_ROWS)
+        w4_rows = w4_scales.rearrange("e a (q r) n -> r q (e a) n", r=SCALE_ROWS)
+        for r in range(SCALE_ROWS):
+            nc.sync.dma_start(out=w4_plane[:].bitcast(I32)[r:P:QUADRANT], in_=w4_rows[r].bitcast(I32))
+            nc.sync.dma_start(out=w8_plane[:].bitcast(I32)[r:P:QUADRANT], in_=w8_rows[r].bitcast(I32))
+
         w8 = []
         w4 = []
-        for g, (e0, e1) in enumerate(runs(LATE_EXPERTS)):
+        for g, (e0, e1) in enumerate(runs(EXPERT_GROUPS)):
             w8_g = keep.tile([P, e1 - e0, 4 * N], U8, name=f"w8_{g}", align_bytes=64)
             w4_g = keep.tile([P, 2 * (e1 - e0), 2 * N], U8, name=f"w4_{g}", align_bytes=64)
             nc.sync.dma_start(
@@ -101,24 +114,28 @@ def tile_moe_ecr_lin_none_kernel(
             )
             w8.append(w8_g)
             w4.append(w4_g)
-        for tile, pos in zip(pos_sb, (pos1, pos2, pos3)):
-            nc.sync.dma_start(tile[:], pos)
-        gates = {}
-        for c, (t0, t1) in enumerate(runs(TOKEN_CHUNKS)):
-            for r in range(TOP):
-                g_sb = keep.tile([P, t1 - t0], F32, name=f"gate{r}_{c}")
-                nc.sync.dma_start(out=g_sb[:], in_=gate[r, :, t0:t1])
-                gates[r, c] = g_sb
 
-        for i, a in enumerate(PASS_ORDER):
-            which, first = plane_of[a]
-            for c, load in enumerate(LOADS[i]):
+        for pos_tile, pos in zip(pos_sb, (pos1, pos2, pos3)):
+            nc.sync.dma_start(pos_tile[:], pos)
+        gates = {}
+        for c, (t0, t1) in enumerate(runs(TOKEN_STEPS)):
+            for r in range(TOP):
+                gate_sb = keep.tile([P, t1 - t0], F32, name=f"gate{r}_{c}")
+                nc.sync.dma_start(out=gate_sb[:], in_=gate[r, :, t0:t1])
+                gates[r, c] = gate_sb
+
+        def gather_slots(dst, src, s0, s1):
+            nc.vector.tensor_copy(dst[:, s0:s1], src[:].indirect(entries(offs_sb, s0, s1)))
+
+        for step, a in enumerate(PASS_ORDER):
+            which, first = PLANE_OF[a]
+            for c, load in enumerate(LOADS[step]):
                 raw, base = raws[a, c]
-                for (engine, width), (u0, u1) in zip(load, runs([w for _, w in load])):
-                    grouped = keep.tile([P, width * PACK], BF16, name=f"grouped{a}_{c}_{u0}", align_bytes=64)
-                    dst = grouped[:].rearrange("p (c i j) -> p c j i", i=4, j=PACK)
-                    src = raw[:, :, u0:u1].rearrange("p j (c i) -> p c j i", i=4)
-                    if engine == "v":
+                for (engine, tokens), (u0, u1) in zip(load, runs([tokens for engine, tokens in load])):
+                    grouped = keep.tile([P, tokens * PACK], BF16, name=f"grouped{a}_{c}_{u0}", align_bytes=64)
+                    dst = grouped[:].rearrange("p (c i j) -> p c j i", i=LINE, j=PACK)
+                    src = raw[:, :, u0:u1].rearrange("p j (c i) -> p c j i", i=LINE)
+                    if engine == "vector":
                         nc.vector.tensor_copy(out=dst, in_=src)
                     else:
                         nc.scalar.copy(out=dst, in_=src)
@@ -127,79 +144,79 @@ def tile_moe_ecr_lin_none_kernel(
                         scales=planes[which][first:P, base + u0 : base + u1],
                         in_=grouped[:],
                     )
-            if i < 2:
+            if step < PASSES - 1:
                 for s0, s1 in runs(EARLY_SLOTS):
-                    gather(slot_codes[a], codes[a], s0, s1)
-            if i == 0:
+                    gather_slots(slot_codes[a], codes[a], s0, s1)
+            if step == 0:
                 for s0, s1 in runs(EARLY_SLOTS):
-                    gather(slot_planes[0], planes[0], s0, s1)
+                    gather_slots(slot_planes[which], planes[which], s0, s1)
 
-        def product(acc, g, e, i):
-            a = PASS_ORDER[i]
-            which, first = plane_of[a]
-            e0 = runs(LATE_EXPERTS)[g][0]
+        def product(acc, g, e, step):
+            a = PASS_ORDER[step]
+            which, first = PLANE_OF[a]
+            place = e - runs(EXPERT_GROUPS)[g][0]
             cols = slice(e * C, (e + 1) * C)
             if a == 0:
-                lhsT = w8[g][:, e - e0, :].bitcast(FP8X4)
-                lhsT_scale = ws[:, e * N : (e + 1) * N]
+                lhsT = w8[g][:, place, :].bitcast(FP8X4)
+                lhsT_scale = w8_plane[:, e, :]
             else:
-                lhsT = w4[g][:, 2 * (e - e0) + a - 1, :].bitcast(FP4X4)
-                lhsT_scale = ws[:, (E + 2 * e + a - 1) * N : (E + 2 * e + a) * N]
+                lhsT = w4[g][:, 2 * place + a - 1, :].bitcast(FP4X4)
+                lhsT_scale = w4_plane[:, 2 * e + a - 1, :]
             nc.tensor.matmul_mx(
                 out=acc,
                 lhsT=lhsT,
                 lhsT_scale=lhsT_scale,
                 rhs=slot_codes[a][:, cols].bitcast(FP8X4),
                 rhs_scale=slot_planes[which][first:P, cols],
-                start=(i == 0),
-                stop=(i == 2),
+                start=(step == 0),
+                stop=(step == PASSES - 1),
             )
 
-        for q in range(1, 4):
-            nc.scalar.dma_start(out=ws_words[32 * q : 32 * q + 4, :], in_=ws_words[4 * q : 4 * q + 4, :])
-
-        last = PASS_ORDER[2]
-        for g, (e0, e1) in enumerate(runs(LATE_EXPERTS)):
-            gather(slot_planes[1], planes[1], e0 * C, e1 * C)
-            gather(slot_codes[last], codes[last], e0 * C, e1 * C)
+        last = PASS_ORDER[PASSES - 1]
+        shared = PLANE_OF[last][0]
+        for g, (e0, e1) in enumerate(runs(EXPERT_GROUPS)):
+            gather_slots(slot_planes[shared], planes[shared], e0 * C, e1 * C)
+            gather_slots(slot_codes[last], codes[last], e0 * C, e1 * C)
             if e1 < E:
                 acc = psum.tile([P, (e1 - e0) * C], F32, name=f"acc{g}", tag="bank")
                 for e in range(e0, e1):
-                    for i in range(3):
-                        product(acc[:, (e - e0) * C : (e - e0 + 1) * C], g, e, i)
+                    for step in range(PASSES):
+                        product(acc[:, (e - e0) * C : (e - e0 + 1) * C], g, e, step)
                 nc.scalar.copy(out=y[:, e0 * C : e1 * C], in_=acc[:])
             else:
                 own = [psum.tile([P, C], F32, name=f"own{e}", tag="bank") for e in range(e0, e1)]
-                for i in range(3):
+                for step in range(PASSES):
                     for e in range(e0, e1):
-                        product(own[e - e0][:], g, e, i)
+                        product(own[e - e0][:], g, e, step)
                 nc.vector.tensor_copy(out=y[:, e0 * C : (e0 + 1) * C], in_=own[0][:])
                 nc.scalar.copy(out=y[:, (e0 + 1) * C : e1 * C], in_=own[1][:])
 
-        def turn(bank, block, r):
-            nc.tensor.matmul(bank, lhsT=block, rhs=ident[:], is_transpose=True, start=(r == 0), stop=(r == TOP - 1))
-
-        for c, (t0, t1) in enumerate(runs(TOKEN_CHUNKS)):
+        for c, (t0, t1) in enumerate(runs(TOKEN_STEPS)):
             width = t1 - t0
             terms = []
             for r in range(TOP):
                 term = keep.tile([P, width], F32, name=f"term{r}_{c}")
-                nc.vector.tensor_tensor(
-                    term[:], y[:].indirect(pos_sb[r][:, t0 // 16 : t1 // 16]), gates[r, c][:], MULT
-                )
+                nc.vector.tensor_tensor(term[:], y[:].indirect(entries(pos_sb[r], t0, t1)), gates[r, c][:], MULT)
                 terms.append(term)
             total = keep.tile([P, width], F32, name=f"total{c}")
             if t1 < T:
-                turned_sb = keep.tile([P, width], F32, name=f"turned_sb{c}")
-                banks = [psum.tile([P, P], F32, name=f"turned{b}", tag="bank") for b in range(width // P)]
+                turned = keep.tile([P, width], F32, name=f"turned{c}")
+                banks = [psum.tile([P, P], F32, name=f"sum{b}", tag="bank") for b in range(width // P)]
                 for r in range(TOP):
                     for b, bank in enumerate(banks):
-                        turn(bank[:], terms[r][:, b * P : (b + 1) * P], r)
+                        nc.tensor.matmul(
+                            bank[:],
+                            lhsT=terms[r][:, b * P : (b + 1) * P],
+                            rhs=ident[:],
+                            is_transpose=True,
+                            start=(r == 0),
+                            stop=(r == TOP - 1),
+                        )
                 for b, bank in enumerate(banks):
-                    nc.scalar.copy(out=turned_sb[:, b * P : (b + 1) * P], in_=bank[:])
+                    nc.scalar.copy(out=turned[:, b * P : (b + 1) * P], in_=bank[:])
                 back = psum.tile([P, width], F32, name="back", tag="bank")
-                for b in range(0, width, P):
-                    nc.tensor.transpose(back[:, b : b + P], turned_sb[:, b : b + P], ident[:])
+                for b in range(len(banks)):
+                    nc.tensor.transpose(back[:, b * P : (b + 1) * P], turned[:, b * P : (b + 1) * P], ident[:])
                 nc.scalar.copy(out=total[:], in_=back[:])
             else:
                 pair = keep.tile([P, width], F32, name="pair")

from contextlib import ExitStack

import concourse.mybir as mybir
from concourse.masks import make_identity

K, T, E, C, N = 1536, 1536, 12, 128, 128
TOP = 3
PAD = 64
S = E * C
P = 128
PACK = 4
K_PASS = P * PACK
PASSES = K // K_PASS
STRIPE = 16
QUADRANT = 32
SCALE_ROWS = 4
LINE = 4
BANKS = 8

F32 = mybir.dt.float32
BF16 = mybir.dt.bfloat16
I32 = mybir.dt.int32
U32 = mybir.dt.uint32
U16 = mybir.dt.uint16
U8 = mybir.dt.uint8
FP8X4 = mybir.dt.float8_e4m3fn_x4
FP4X4 = mybir.dt.float4_e2m1fn_x4
MULT = mybir.AluOpType.mult
ADD = mybir.AluOpType.add

FLOPS = 2 * K * S * N

PASS_ORDER = (1, 0, 2)
PLANE_OF = {1: (0, 0), 0: (1, SCALE_ROWS), 2: (1, 0)}

LOADS = (
    ((("vector", 512), ("scalar", 256)), (("vector", 256), ("scalar", 256)), (("vector", 128), ("scalar", 128))),
    ((("scalar", 512),), (("scalar", 512),), (("scalar", 256), ("scalar", 256))),
    ((("scalar", 512),), (("scalar", 512),), (("vector", 256), ("scalar", 256))),
)
EARLY_SLOTS = (S // 2, S // 2)
EXPERT_GROUPS = (4, 4, 2, 2)
TOKEN_STEPS = (512, 512, 256, 256)


def runs(sizes):
    start = 0
    result = []
    for size in sizes:
        result.append((start, start + size))
        start = start + size
    return result


def entries(list_tile, start, stop):
    return list_tile[:, start // STRIPE : stop // STRIPE]


def tile_moe_ecr_lin_none_kernel(
    tc, xT, w8_words, w8_scales, w4_words, w4_scales, gate, offs, pos1, pos2, pos3, out
):
    nc = tc.nc
    with ExitStack() as ctx:
        lists = ctx.enter_context(tc.tile_pool(name="lists", bufs=1))
        keep = ctx.enter_context(tc.tile_pool(name="keep", bufs=1))
        psum = ctx.enter_context(tc.psum_pool(name="psum", bufs=BANKS))

        w8_plane = keep.tile([P, E, N], U8, name="w8_plane", align_bytes=64)
        w4_plane = keep.tile([P, 2 * E, N], U8, name="w4_plane", align_bytes=64)
        planes = [keep.tile([P, T], U8, name=f"plane{i}", align_bytes=64) for i in range(2)]
        y = keep.tile([P, S + PAD], F32, name="y")
        nc.vector.memset(w4_plane[:].bitcast(I32), 0)
        nc.vector.memset(w8_plane[:].bitcast(I32), 0)
        for plane in planes:
            nc.vector.memset(plane[:].bitcast(I32), 0)
        nc.vector.memset(y[:, S:], 0.0)

        ident = keep.tile([P, P], F32, name="ident")
        make_identity(nc, ident[:])

        codes = [keep.tile([P, T], U32, name=f"codes{a}", align_bytes=64) for a in range(PASSES)]
        slot_codes = [keep.tile([P, S], U32, name=f"slot_codes{a}", align_bytes=64) for a in range(PASSES)]
        slot_planes = [keep.tile([P, S], U8, name=f"slot_plane{i}", align_bytes=64) for i in range(2)]
        offs_sb = lists.tile([P, S // STRIPE], U16, name="offs_sb")
        pos_sb = [lists.tile([P, T // STRIPE], U16, name=f"pos_sb{r}") for r in range(TOP)]

        raws = {}
        for step, a in enumerate(PASS_ORDER):
            rows = xT[a * K_PASS : (a + 1) * K_PASS, :].rearrange("(p j) t -> p j t", j=PACK)
            sizes = [sum(tokens for engine, tokens in load) for load in LOADS[step]]
            for c, (t0, t1) in enumerate(runs(sizes)):
                raw = keep.tile([P, PACK, t1 - t0], F32, name=f"raw{a}_{c}")
                nc.sync.dma_start(out=raw[:], in_=rows[:, :, t0:t1])
                raws[a, c] = (raw, t0)
            if step == 0:
                nc.sync.dma_start(offs_sb[:], offs)

        w8_rows = w8_scales.rearrange("e a (q r) n -> r q (e a) n", r=SCALE_ROWS)
        w4_rows = w4_scales.rearrange("e a (q r) n -> r q (e a) n", r=SCALE_ROWS)
        for r in range(SCALE_ROWS):
            nc.sync.dma_start(out=w4_plane[:].bitcast(I32)[r:P:QUADRANT], in_=w4_rows[r].bitcast(I32))
            nc.sync.dma_start(out=w8_plane[:].bitcast(I32)[r:P:QUADRANT], in_=w8_rows[r].bitcast(I32))

        w8 = []
        w4 = []
        for g, (e0, e1) in enumerate(runs(EXPERT_GROUPS)):
            w8_g = keep.tile([P, e1 - e0, 4 * N], U8, name=f"w8_{g}", align_bytes=64)
            w4_g = keep.tile([P, 2 * (e1 - e0), 2 * N], U8, name=f"w4_{g}", align_bytes=64)
            nc.sync.dma_start(
                out=w4_g[:].bitcast(I32), in_=w4_words[e0:e1].rearrange("e a p b -> p (e a) b").bitcast(I32)
            )
            nc.sync.dma_start(
                out=w8_g[:].bitcast(I32), in_=w8_words[e0:e1].rearrange("e a p n r -> p (e a) (n r)").bitcast(I32)
            )
            w8.append(w8_g)
            w4.append(w4_g)

        for pos_tile, pos in zip(pos_sb, (pos1, pos2, pos3)):
            nc.sync.dma_start(pos_tile[:], pos)
        gates = {}
        for c, (t0, t1) in enumerate(runs(TOKEN_STEPS)):
            for r in range(TOP):
                gate_sb = keep.tile([P, t1 - t0], F32, name=f"gate{r}_{c}")
                nc.sync.dma_start(out=gate_sb[:], in_=gate[r, :, t0:t1])
                gates[r, c] = gate_sb

        def gather_slots(dst, src, s0, s1):
            nc.vector.tensor_copy(dst[:, s0:s1], src[:].indirect(entries(offs_sb, s0, s1)))

        for step, a in enumerate(PASS_ORDER):
            which, first = PLANE_OF[a]
            for c, load in enumerate(LOADS[step]):
                raw, base = raws[a, c]
                for (engine, tokens), (u0, u1) in zip(load, runs([tokens for engine, tokens in load])):
                    grouped = keep.tile([P, tokens * PACK], BF16, name=f"grouped{a}_{c}_{u0}", align_bytes=64)
                    dst = grouped[:].rearrange("p (c i j) -> p c j i", i=LINE, j=PACK)
                    src = raw[:, :, u0:u1].rearrange("p j (c i) -> p c j i", i=LINE)
                    if engine == "vector":
                        nc.vector.tensor_copy(out=dst, in_=src)
                    else:
                        nc.scalar.copy(out=dst, in_=src)
                    nc.vector.quantize_mx(
                        out=codes[a][:, base + u0 : base + u1].bitcast(FP8X4),
                        scales=planes[which][first:P, base + u0 : base + u1],
                        in_=grouped[:],
                    )
            if step < PASSES - 1:
                for s0, s1 in runs(EARLY_SLOTS):
                    gather_slots(slot_codes[a], codes[a], s0, s1)
            if step == 0:
                for s0, s1 in runs(EARLY_SLOTS):
                    gather_slots(slot_planes[which], planes[which], s0, s1)

        def product(acc, g, e, step):
            a = PASS_ORDER[step]
            which, first = PLANE_OF[a]
            place = e - runs(EXPERT_GROUPS)[g][0]
            cols = slice(e * C, (e + 1) * C)
            if a == 0:
                lhsT = w8[g][:, place, :].bitcast(FP8X4)
                lhsT_scale = w8_plane[:, e, :]
            else:
                lhsT = w4[g][:, 2 * place + a - 1, :].bitcast(FP4X4)
                lhsT_scale = w4_plane[:, 2 * e + a - 1, :]
            nc.tensor.matmul_mx(
                out=acc,
                lhsT=lhsT,
                lhsT_scale=lhsT_scale,
                rhs=slot_codes[a][:, cols].bitcast(FP8X4),
                rhs_scale=slot_planes[which][first:P, cols],
                start=(step == 0),
                stop=(step == PASSES - 1),
            )

        last = PASS_ORDER[PASSES - 1]
        shared = PLANE_OF[last][0]
        for g, (e0, e1) in enumerate(runs(EXPERT_GROUPS)):
            gather_slots(slot_planes[shared], planes[shared], e0 * C, e1 * C)
            gather_slots(slot_codes[last], codes[last], e0 * C, e1 * C)
            if e1 < E:
                acc = psum.tile([P, (e1 - e0) * C], F32, name=f"acc{g}", tag="bank")
                for e in range(e0, e1):
                    for step in range(PASSES):
                        product(acc[:, (e - e0) * C : (e - e0 + 1) * C], g, e, step)
                nc.scalar.copy(out=y[:, e0 * C : e1 * C], in_=acc[:])
            else:
                own = [psum.tile([P, C], F32, name=f"own{e}", tag="bank") for e in range(e0, e1)]
                for step in range(PASSES):
                    for e in range(e0, e1):
                        product(own[e - e0][:], g, e, step)
                nc.vector.tensor_copy(out=y[:, e0 * C : (e0 + 1) * C], in_=own[0][:])
                nc.scalar.copy(out=y[:, (e0 + 1) * C : e1 * C], in_=own[1][:])

        for c, (t0, t1) in enumerate(runs(TOKEN_STEPS)):
            width = t1 - t0
            terms = []
            for r in range(TOP):
                term = keep.tile([P, width], F32, name=f"term{r}_{c}")
                nc.vector.tensor_tensor(term[:], y[:].indirect(entries(pos_sb[r], t0, t1)), gates[r, c][:], MULT)
                terms.append(term)
            total = keep.tile([P, width], F32, name=f"total{c}")
            if t1 < T:
                turned = keep.tile([P, width], F32, name=f"turned{c}")
                banks = [psum.tile([P, P], F32, name=f"sum{b}", tag="bank") for b in range(width // P)]
                for r in range(TOP):
                    for b, bank in enumerate(banks):
                        nc.tensor.matmul(
                            bank[:],
                            lhsT=terms[r][:, b * P : (b + 1) * P],
                            rhs=ident[:],
                            is_transpose=True,
                            start=(r == 0),
                            stop=(r == TOP - 1),
                        )
                for b, bank in enumerate(banks):
                    nc.scalar.copy(out=turned[:, b * P : (b + 1) * P], in_=bank[:])
                back = psum.tile([P, width], F32, name="back", tag="bank")
                for b in range(len(banks)):
                    nc.tensor.transpose(back[:, b * P : (b + 1) * P], turned[:, b * P : (b + 1) * P], ident[:])
                nc.scalar.copy(out=total[:], in_=back[:])
            else:
                pair = keep.tile([P, width], F32, name="pair")
                nc.vector.tensor_tensor(pair[:], terms[0][:], terms[1][:], ADD)
                nc.vector.tensor_tensor(total[:], pair[:], terms[2][:], ADD)
            nc.sync.dma_start(out=out[:, t0:t1], in_=total[:])
